import numpy as np
import ml_dtypes


def mxq(x, axis, fmt="e4m3"):
    dtype, down = {"e4m3": (ml_dtypes.float8_e4m3fn, 7), "e5m2": (ml_dtypes.float8_e5m2, 14)}[fmt]
    v = np.moveaxis(np.asarray(x, np.float32).astype(ml_dtypes.bfloat16).astype(np.float64), axis, -1)
    blocks = v.reshape(v.shape[:-1] + (-1, 32))
    amax = np.abs(blocks).max(-1, keepdims=True)
    byte = np.maximum(np.where(amax > 0, np.frexp(amax)[1] - 1 + 127, 0) - down, 1)
    scale = np.exp2(byte - 127.0)
    codes = (blocks / scale).astype(np.float32).astype(dtype).astype(np.float64)
    return np.moveaxis((codes * scale).reshape(v.shape), -1, axis)


WIDE = False


def mx_kscale(k):
    if not WIDE:
        return np.ones(k)
    levels = np.array([10, -10, 5, -5, 0])
    if k % 512:
        return np.exp2(np.random.permutation(np.resize(levels, k // 32))).repeat(32)
    a = np.empty((k // 512, 16))
    for p in range(k // 512):
        a[p, :8] = np.random.permutation(np.resize(levels, 8))
        for g in range(8):
            far = levels[np.abs(levels - a[p, g]) >= 10]
            a[p, g + 8] = far[np.random.randint(len(far))]
    return np.exp2(a.ravel()).repeat(32)


def f64(x):
    return np.asarray(x).astype(np.float64)


def striped(idx):
    return np.tile(np.asarray(idx).reshape(-1, 16).T, (8, 1)).astype(np.uint16)


def unstriped(offs):
    return offs[:16].T.reshape(-1).astype(np.int64)


E2M1 = np.array([0.0, 0.5, 1.0, 1.5, 2.0, 3.0, 4.0, 6.0, -0.0, -0.5, -1.0, -1.5, -2.0, -3.0, -4.0, -6.0])


def pack_weight(w, fmt):
    k, n = w.shape
    w = f64(np.asarray(w, np.float32).astype(ml_dtypes.bfloat16)).reshape(k // 32, 32, n)
    amax = np.abs(w).max(1)
    if fmt == "e4m3":
        byte = np.frexp(amax)[1] - 1 + 127 - 7
    else:
        mant, ex = np.frexp(amax / 6.0)
        byte = np.where(mant > 0.5, ex, ex - 1) + 127
    byte = np.clip(np.where(amax > 0, byte, 1), 1, 254)
    scaled = (w * np.exp2(127.0 - byte)[:, None, :]).reshape(k, n).astype(np.float32)
    by_word = np.ascontiguousarray(scaled.reshape(k // 512, 128, 4, n).transpose(0, 1, 3, 2))
    if fmt == "e4m3":
        words = by_word.astype(ml_dtypes.float8_e4m3fn).view(np.uint8)
    else:
        c = by_word.astype(ml_dtypes.float4_e2m1fn).view(np.uint8) & 0xF
        words = (c[..., 0::2] | (c[..., 1::2] << 4)).reshape(k // 512, 128, 2 * n)
    return np.ascontiguousarray(words), np.ascontiguousarray(byte.astype(np.uint8).reshape(k // 512, 16, n))


def unpack_weight(words, scales, fmt):
    g, _, n = scales.shape
    words = np.ascontiguousarray(words).reshape(g, 128, n, -1)
    if fmt == "e4m3":
        vals = words.view(ml_dtypes.float8_e4m3fn).astype(np.float64)
    else:
        nib = np.empty((g, 128, n, 4), np.uint8)
        nib[..., 0::2] = words & 0xF
        nib[..., 1::2] = words >> 4
        vals = E2M1[nib]
    vals = vals * np.repeat(np.exp2(scales.astype(np.float64) - 127.0), 8, axis=1)[..., None]
    return vals.transpose(0, 1, 3, 2).reshape(g * 512, n)


D, E, T, I, Q, U = 512, 512, 1024, 256, 512, 1024


def setup_inputs():
    n = np.random.standard_normal
    idx = np.random.permutation(T)[:I]
    idx4 = np.random.permutation(U)[:I]
    fd = mx_kscale(D)
    fe = mx_kscale(E)
    fq = mx_kscale(Q)
    keysp = pack_weight(n((D, T)) / fd[:, None], "e4m3")
    valsp = pack_weight(n((E, T)) / fe[:, None], "e4m3")
    return {
        "query": (n((D, Q)) * 1.0 / np.sqrt(D) * fd[:, None]).astype(np.float32),
        "keys_words": keysp[0],
        "keys_scales": keysp[1],
        "floor": (np.random.uniform(0.05, 0.3, (Q, 1))).astype(np.float32),
        "reserve": (np.random.uniform(20.0, 100.0, (Q, 1))).astype(np.float32),
        "gout": (n((E, Q)) * 1 / np.sqrt(E) * fe[:, None]).astype(np.float32),
        "vals_words": valsp[0],
        "vals_scales": valsp[1],
        "qs": (np.random.uniform(100.0, 400.0, (Q, 1)) * fq[:, None]).astype(np.float32),
        "qrows": (n((Q, D)) / fq[:, None]).astype(np.float32),
        "old": (n((D, U)) * 4.0).astype(np.float32),
        "fade": (np.random.uniform(0.5, 1.0, (1, U))).astype(np.float32),
        "offs": striped(idx),
        "offs4": striped(idx4),
    }


def reference(query, keys_words, keys_scales, floor, reserve, gout, vals_words, vals_scales, qs, qrows, old, fade, offs, offs4):
    idx = unstriped(offs)
    idx4 = unstriped(offs4)
    keysu = unpack_weight(keys_words, keys_scales, "e4m3")
    valsu = unpack_weight(vals_words, vals_scales, "e4m3")
    queryq = mxq(f64(query), 0, "e4m3")
    keysidxg = keysu[:, idx]
    a = queryq.T @ keysidxg
    p = np.square(a) + f64(floor)
    z = np.sum(p, axis=1, keepdims=True) + f64(reserve)
    goutq = mxq(f64(gout), 0, "e4m3")
    valsidxg = valsu[:, idx]
    c0 = goutq.T @ valsidxg
    dz = np.sum(c0 * p / np.square(z) * (-1.0), axis=1, keepdims=True)
    dp = c0 / z + dz
    da = dp * a * 2.0
    gs = da * f64(qs)
    qrowsq = mxq(f64(qrows), 0, "e4m3")
    gsq = mxq(gs, 0, "e4m3")
    gk = qrowsq.T @ gsq
    gf = np.zeros((D, U))
    gf[:, idx4] = gk
    y = f64(old) * f64(fade) + gf
    return y

@@ -1,0 +1,242 @@
+from contextlib import ExitStack
+
+import concourse.mybir as mybir
+from concourse.masks import make_identity
+
+F32 = mybir.dt.float32
+BF16 = mybir.dt.bfloat16
+I32 = mybir.dt.int32
+U32 = mybir.dt.uint32
+U16 = mybir.dt.uint16
+U8 = mybir.dt.uint8
+FP8X4 = mybir.dt.float8_e4m3fn_x4
+ALU = mybir.AluOpType
+ACT = mybir.ActivationFunctionType
+
+D, E, T, I, Q, U = 512, 512, 1024, 256, 512, 1024
+P = 128
+PACK = 4
+FLOPS = 2 * Q * I * (D + E + D)
+
+
+def tile_attend_bsquareshares_k_kernel(tc, query, keys_words, keys_scales, floor, reserve, gout,
+                                        vals_words, vals_scales, qs, qrows, old, fade, offs, offs4, out):
+    nc = tc.nc
+    with ExitStack() as ctx:
+        sb = ctx.enter_context(tc.tile_pool(name="sb", bufs=1))
+        ps = ctx.enter_context(tc.psum_pool(name="ps", bufs=1))
+
+        def sbt(shape, dtype, name):
+            return sb.tile(shape, dtype, name=name, align_bytes=64)
+
+        slots = sbt([P, I // 16], U16, "slots")
+        places = sbt([P, I // 16], U16, "places")
+        key_pool = sbt([P, T], I32, "key_pool")
+        val_pool = sb.tile([P, T], I32, name="val_pool", tag="val_pool", align_bytes=64)
+        key_bytes = sbt([P, T], U8, "key_bytes")
+        val_bytes = sbt([P, T], U8, "val_bytes")
+        nc.gpsimd.memset(key_bytes[:].bitcast(I32), 0)
+        nc.gpsimd.memset(val_bytes[:].bitcast(I32), 0)
+        fade_rows = sbt([P, P], F32, "fade_rows")
+        nc.gpsimd.memset(fade_rows[:], 0.0)
+
+        def load_words(pool_tile, words):
+            nc.sync.dma_start(out=pool_tile[:], in_=words[0].rearrange("p n t -> p (n t)").bitcast(I32))
+
+        def load_bytes(byte_tile, scales):
+            for quad in range(4):
+                nc.sync.dma_start(out=byte_tile[32 * quad:32 * quad + 4, :].bitcast(I32),
+                                  in_=scales[0, 4 * quad:4 * quad + 4, :].bitcast(I32))
+
+        def load_half(src, name, h):
+            raw = sbt([P, PACK, 256], F32, "%s_raw%d" % (name, h))
+            nc.sync.dma_start(out=raw[:], in_=src.rearrange("(p j) c -> p j c", j=PACK)[:, :, 256 * h:256 * h + 256])
+            return raw
+
+        nc.sync.dma_start(slots[:], offs)
+        query_raw = [load_half(query, "query", 0)]
+        load_bytes(key_bytes, keys_scales)
+        query_raw.append(load_half(query, "query", 1))
+        load_words(key_pool, keys_words)
+        gout_raw = [load_half(gout, "gout", 0)]
+        load_bytes(val_bytes, vals_scales)
+        gout_raw.append(load_half(gout, "gout", 1))
+        load_words(val_pool, vals_words)
+        row_vec = {}
+        for name, src in (("floor", floor), ("reserve", reserve), ("qs", qs)):
+            v = sbt([P, PACK], F32, name + "_sb")
+            nc.gpsimd.dma_start(out=v[:], in_=src.rearrange("(p r) o -> p (r o)", r=PACK))
+            row_vec[name] = v
+        qrows_raw = [load_half(qrows, "qrows", h) for h in range(2)]
+        nc.gpsimd.dma_start(out=fade_rows[0:U // P, :], in_=fade.rearrange("o (c n) -> (o c) n", n=P))
+        nc.sync.dma_start(places[:], offs4)
+        old_sb = []
+        for j in range(4):
+            o = sbt([P, U], F32, "old%d" % j)
+            nc.sync.dma_start(out=o[:], in_=old[P * j:P * j + P, :])
+            old_sb.append(o)
+
+        ident = sbt([P, P], F32, "ident")
+        make_identity(nc, ident[:])
+
+        windows = []
+        for j in range(2):
+            w = sbt([P, U], F32, "window%d" % j)
+            nc.vector.memset(w[:], 0.0)
+            windows.append(w)
+
+        def gather(window, dtype, name):
+            picked = sbt([P, I], dtype, name)
+            nc.vector.tensor_copy(picked[:], window.indirect(slots[:]))
+            return picked
+
+        def dealt_views(bf, raw, h):
+            dst = bf[:].rearrange("p (r s j) -> p s r j", r=PACK, j=PACK)[:, 64 * h:64 * h + 64, :, :]
+            src = raw[:].rearrange("p j (s r) -> p s r j", r=PACK)
+            return dst, src
+
+        def quantise(bf, name, width):
+            words = sbt([P, width], U32, name + "_words")
+            scales = sbt([P, width], U8, name + "_scales")
+            nc.vector.quantize_mx(out=words[:].bitcast(FP8X4), scales=scales[:], in_=bf)
+            return words, scales
+
+        key_scales = gather(key_bytes[:], U8, "key_scales")
+        query_bf = sbt([P, Q * PACK], BF16, "query_bf")
+        nc.scalar.copy(*dealt_views(query_bf, query_raw[0], 0))
+        nc.vector.tensor_copy(*dealt_views(query_bf, query_raw[1], 1))
+        query_words, query_scales = quantise(query_bf[:], "query", Q)
+        key_words = gather(key_pool[:].bitcast(U32), U32, "key_words")
+
+        score = []
+        for h in range(2):
+            bank = ps.tile([P, PACK, P], F32, name="score%d" % h, tag="score", bufs=2)
+            for r in range(PACK):
+                nc.tensor.matmul_mx(out=bank[:, r, :],
+                                    lhsT=query_words[:, P * r:P * r + P].bitcast(FP8X4),
+                                    lhsT_scale=query_scales[:, P * r:P * r + P],
+                                    rhs=key_words[:, P * h:P * h + P].bitcast(FP8X4),
+                                    rhs_scale=key_scales[:, P * h:P * h + P], start=True, stop=True)
+            score.append(bank)
+
+        z_parts = sbt([P, 3, PACK], F32, "z_parts")
+        floors = sbt([P, PACK], F32, "floors")
+        nc.gpsimd.tensor_scalar(floors[:], row_vec["floor"][:], float(I), 0.0, ALU.mult, ALU.add)
+        nc.gpsimd.tensor_tensor(z_parts[:, 2, :], floors[:], row_vec["reserve"][:], ALU.add)
+        squares = sbt([P, PACK, I], F32, "squares")
+        for h in range(2):
+            for r in range(PACK):
+                nc.scalar.activation(squares[:, r, P * h:P * h + P], score[h][:, r, :], ACT.Square,
+                                     accum_out=z_parts[:, h, r:r + 1])
+
+        gout_bf = sbt([P, Q * PACK], BF16, "gout_bf")
+        nc.vector.tensor_copy(*dealt_views(gout_bf, gout_raw[0], 0))
+        val_scales = gather(val_bytes[:], U8, "val_scales")
+        nc.vector.tensor_copy(*dealt_views(gout_bf, gout_raw[1], 1))
+        gout_words, gout_scales = quantise(gout_bf[:], "gout", Q)
+
+        inv_z = sbt([P, PACK], F32, "inv_z")
+        alpha = sbt([P, PACK], F32, "alpha")
+        gamma = sbt([P, PACK], F32, "gamma")
+        val_words = gather(val_pool[:].bitcast(U32), U32, "val_words")
+        z = sb.tile([P, PACK], F32, name="z", tag="val_pool", align_bytes=64)
+        nc.vector.tensor_reduce(z[:], z_parts[:].rearrange("p t r -> p r t"), mybir.AxisListType.X, ALU.add)
+        nc.vector.reciprocal(inv_z[:], z[:])
+        nc.vector.scalar_tensor_tensor(out=alpha[:], in0=row_vec["qs"][:], scalar=2.0, in1=inv_z[:],
+                                       op0=ALU.mult, op1=ALU.mult)
+        nc.vector.scalar_tensor_tensor(out=gamma[:], in0=alpha[:], scalar=-1.0, in1=inv_z[:],
+                                       op0=ALU.mult, op1=ALU.mult)
+
+        qrows_bf = sbt([P, D * PACK], BF16, "qrows_bf")
+
+        def cast_qrows(h):
+            dst = qrows_bf[:, 1024 * h:1024 * h + 1024].rearrange("p (c i t) -> p c t i", i=4, t=PACK)
+            src = qrows_raw[h][:].rearrange("p t (c i) -> p c t i", i=4)
+            nc.scalar.copy(dst, src)
+
+        cast_qrows(0)
+
+        weighted = sbt([P, PACK, I], F32, "weighted")
+        total = sbt([P, PACK], F32, "total")
+        beta = sbt([P, PACK], F32, "beta")
+        slope = sbt([P, PACK, I], F32, "slope")
+        for r in range(PACK):
+            c0 = ps.tile([P, I], F32, name="c0_%d" % r, tag="wide", bufs=4)
+            nc.tensor.matmul_mx(out=c0[:], lhsT=gout_words[:, P * r:P * r + P].bitcast(FP8X4),
+                                lhsT_scale=gout_scales[:, P * r:P * r + P],
+                                rhs=val_words[:].bitcast(FP8X4), rhs_scale=val_scales[:], start=True, stop=True)
+            nc.vector.scalar_tensor_tensor(out=weighted[:, r, :], in0=squares[:, r, :],
+                                           scalar=row_vec["floor"][:, r:r + 1], in1=c0[:],
+                                           op0=ALU.add, op1=ALU.mult, accum_out=total[:, r:r + 1])
+            nc.scalar.activation(beta[:, r:r + 1], total[:, r:r + 1], ACT.Copy, scale=gamma[:, r:r + 1])
+            nc.scalar.activation(slope[:, r, :], c0[:], ACT.Identity, bias=beta[:, r:r + 1],
+                                 scale=alpha[:, r:r + 1])
+
+        qrows_q = [quantise(qrows_bf[:, 0:1024], "qrows0", 256)]
+        gs_bf = sbt([P, I * PACK], BF16, "gs_bf")
+        for h in range(2):
+            nc.vector.tensor_tensor(out=gs_bf[:, 512 * h:512 * h + 512].rearrange("p (i r) -> p i r", r=PACK),
+                                    in0=score[h][:].rearrange("p r i -> p i r"),
+                                    in1=slope[:, :, P * h:P * h + P].rearrange("p r i -> p i r"), op=ALU.mult)
+        gs_words, gs_scales = quantise(gs_bf[:], "gs", I)
+        cast_qrows(1)
+
+        fade_ps = ps.tile([P, P], F32, name="fade_ps", tag="back", bufs=2)
+        nc.tensor.transpose(fade_ps[:], fade_rows[:], ident[:])
+        fade_col = sbt([P, U // P], F32, "fade_col")
+        nc.scalar.copy(fade_col[:], fade_ps[:, 0:U // P])
+
+        faded = [[None] * (U // P) for pair in range(2)]
+
+        def fade_pair(pair):
+            for c2 in range(U // P // 2):
+                bank = ps.tile([P, 2, 2, P], F32, name="turn%d_%d" % (pair, c2), tag="wide", bufs=4)
+                for cc in range(2):
+                    c = 2 * c2 + cc
+                    for jj in range(2):
+                        nc.tensor.transpose(bank[:, cc, jj, :], old_sb[2 * pair + jj][:, P * c:P * c + P], ident[:])
+                for cc in range(2):
+                    c = 2 * c2 + cc
+                    f = sbt([P, 2 * P], F32, "faded%d_%d" % (pair, c))
+                    nc.scalar.activation(f[:], bank[:, cc, :, :].rearrange("p j d -> p (j d)"), ACT.Copy,
+                                         scale=fade_col[:, c:c + 1])
+                    faded[pair][c] = f
+
+        def key_grad(j):
+            words, scales = qrows_q[j // 2]
+            cols = slice(P * (j % 2), P * (j % 2) + P)
+            bank = ps.tile([P, I], F32, name="gk_ps%d" % j, tag="score", bufs=2)
+            nc.tensor.matmul_mx(out=bank[:], lhsT=words[:, cols].bitcast(FP8X4), lhsT_scale=scales[:, cols],
+                                rhs=gs_words[:].bitcast(FP8X4), rhs_scale=gs_scales[:], start=True, stop=True)
+            gk = sbt([P, I], F32, "gk%d" % j)
+            nc.scalar.copy(gk[:], bank[:])
+            return gk
+
+        def scatter(j):
+            nc.vector.tensor_copy(windows[j % 2][:].indirect(places[:]), gks[j][:])
+
+        def finish(j):
+            for half in range(2):
+                bank = ps.tile([P, PACK, P], F32, name="back%d_%d" % (j, half), tag="back" if j < 2 else "wide",
+                               bufs=2 if j < 2 else 4)
+                for cc in range(PACK):
+                    nc.tensor.transpose(bank[:, cc, :], faded[j // 2][PACK * half + cc][:, P * (j % 2):P * (j % 2) + P],
+                                        ident[:])
+                res = sbt([P, 512], F32, "res%d_%d" % (j, half))
+                nc.vector.tensor_tensor(out=res[:], in0=bank[:].rearrange("p c n -> p (c n)"),
+                                        in1=windows[j % 2][:, 512 * half:512 * half + 512], op=ALU.add)
+                nc.sync.dma_start(out=out[P * j:P * j + P, 512 * half:512 * half + 512], in_=res[:])
+
+        gks = [key_grad(0), key_grad(1)]
+        fade_pair(0)
+        scatter(0)
+        qrows_q.append(quantise(qrows_bf[:, 1024:2048], "qrows1", 256))
+        scatter(1)
+        gks.extend([key_grad(2), key_grad(3)])
+        finish(0)
+        fade_pair(1)
+        scatter(2)
+        finish(1)
+        scatter(3)
+        finish(2)
+        finish(3)

@@ -26,13 +26,13 @@ def tile_attend_bsquareshares_k_kernel(tc, query, keys_words, keys_scales, floor
         sb = ctx.enter_context(tc.tile_pool(name="sb", bufs=1))
         ps = ctx.enter_context(tc.psum_pool(name="ps", bufs=1))
 
-        def sbt(shape, dtype, name):
-            return sb.tile(shape, dtype, name=name, align_bytes=64)
+        def sbt(shape, dtype, name, after=None):
+            return sb.tile(shape, dtype, name=name, tag=after or name, align_bytes=64)
 
         slots = sbt([P, I // 16], U16, "slots")
         places = sbt([P, I // 16], U16, "places")
         key_pool = sbt([P, T], I32, "key_pool")
-        val_pool = sb.tile([P, T], I32, name="val_pool", tag="val_pool", align_bytes=64)
+        val_pool = sbt([P, T], I32, "val_pool")
         key_bytes = sbt([P, T], U8, "key_bytes")
         val_bytes = sbt([P, T], U8, "val_bytes")
         nc.gpsimd.memset(key_bytes[:].bitcast(I32), 0)
@@ -58,35 +58,39 @@ def tile_attend_bsquareshares_k_kernel(tc, query, keys_words, keys_scales, floor
         load_bytes(key_bytes, keys_scales)
         query_raw.append(load_half(query, "query", 1))
         load_words(key_pool, keys_words)
-        gout_raw = [load_half(gout, "gout", 0)]
-        load_bytes(val_bytes, vals_scales)
-        gout_raw.append(load_half(gout, "gout", 1))
+        gout_raw = [load_half(gout, "gout", h) for h in range(2)]
         load_words(val_pool, vals_words)
-        row_vec = {}
-        for name, src in (("floor", floor), ("reserve", reserve), ("qs", qs)):
-            v = sbt([P, PACK], F32, name + "_sb")
-            nc.gpsimd.dma_start(out=v[:], in_=src.rearrange("(p r) o -> p (r o)", r=PACK))
-            row_vec[name] = v
+        load_bytes(val_bytes, vals_scales)
+
+        def load_rows(queue, src, name):
+            v = sbt([P, PACK], F32, name)
+            queue.dma_start(out=v[:], in_=src.rearrange("(p r) o -> p (r o)", r=PACK))
+            return v
+
+        qs_sb = load_rows(nc.sync, qs, "qs_sb")
         qrows_raw = [load_half(qrows, "qrows", h) for h in range(2)]
-        nc.gpsimd.dma_start(out=fade_rows[0:U // P, :], in_=fade.rearrange("o (c n) -> (o c) n", n=P))
-        nc.sync.dma_start(places[:], offs4)
         old_sb = []
         for j in range(4):
             o = sbt([P, U], F32, "old%d" % j)
             nc.sync.dma_start(out=o[:], in_=old[P * j:P * j + P, :])
             old_sb.append(o)
+            if j == 1:
+                nc.sync.dma_start(places[:], offs4)
 
+        nc.gpsimd.dma_start(out=fade_rows[0:U // P, :], in_=fade.rearrange("o (c n) -> (o c) n", n=P))
         ident = sbt([P, P], F32, "ident")
         make_identity(nc, ident[:])
+        floor_sb = load_rows(nc.gpsimd, floor, "floor_sb")
+        reserve_sb = load_rows(nc.gpsimd, reserve, "reserve_sb")
 
         windows = []
-        for j in range(2):
+        for j in range(4):
             w = sbt([P, U], F32, "window%d" % j)
             nc.vector.memset(w[:], 0.0)
             windows.append(w)
 
-        def gather(window, dtype, name):
-            picked = sbt([P, I], dtype, name)
+        def gather(window, dtype, name, after=None):
+            picked = sbt([P, I], dtype, name, after)
             nc.vector.tensor_copy(picked[:], window.indirect(slots[:]))
             return picked
 
@@ -121,30 +125,49 @@ def tile_attend_bsquareshares_k_kernel(tc, query, keys_words, keys_scales, floor
 
         z_parts = sbt([P, 3, PACK], F32, "z_parts")
         floors = sbt([P, PACK], F32, "floors")
-        nc.gpsimd.tensor_scalar(floors[:], row_vec["floor"][:], float(I), 0.0, ALU.mult, ALU.add)
-        nc.gpsimd.tensor_tensor(z_parts[:, 2, :], floors[:], row_vec["reserve"][:], ALU.add)
+        nc.gpsimd.tensor_scalar(floors[:], floor_sb[:], float(I), 0.0, ALU.mult, ALU.add)
+        nc.gpsimd.tensor_tensor(z_parts[:, 2, :], floors[:], reserve_sb[:], ALU.add)
         squares = sbt([P, PACK, I], F32, "squares")
         for h in range(2):
             for r in range(PACK):
                 nc.scalar.activation(squares[:, r, P * h:P * h + P], score[h][:, r, :], ACT.Square,
                                      accum_out=z_parts[:, h, r:r + 1])
 
-        gout_bf = sbt([P, Q * PACK], BF16, "gout_bf")
+        fade_ps = ps.tile([P, P], F32, name="fade_ps", tag="back", bufs=2)
+        nc.tensor.transpose(fade_ps[:], fade_rows[:], ident[:])
+        fade_col = sbt([P, U // P], F32, "fade_col", after="key_words")
+        nc.scalar.copy(fade_col[:], fade_ps[:, 0:U // P])
+
+        fade_all = sbt([P, U], F32, "fade_all")
+        for half in range(2):
+            bank = ps.tile([P, PACK, P], F32, name="spread%d" % half, tag="back", bufs=2)
+            for cc in range(PACK):
+                c = PACK * half + cc
+                nc.tensor.transpose(bank[:, cc, :], fade_col[:, c:c + 1].to_broadcast([P, P]), ident[:])
+            nc.scalar.copy(fade_all[:, 512 * half:512 * half + 512], bank[:].rearrange("p c n -> p (c n)"))
+
+        minus_two_qs = sbt([P, PACK], F32, "minus_two_qs")
+        nc.gpsimd.tensor_scalar(minus_two_qs[:], qs_sb[:], -2.0, 0.0, ALU.mult, ALU.add)
+        parts = sbt([P, PACK, I], F32, "parts")
+        for r in range(PACK):
+            nc.gpsimd.tensor_scalar(parts[:, r, :], squares[:, r, :], floor_sb[:, r:r + 1], minus_two_qs[:, r:r + 1],
+                                    ALU.add, ALU.mult)
+
+        gout_bf = sbt([P, Q * PACK], BF16, "gout_bf", after="key_pool")
         nc.vector.tensor_copy(*dealt_views(gout_bf, gout_raw[0], 0))
-        val_scales = gather(val_bytes[:], U8, "val_scales")
         nc.vector.tensor_copy(*dealt_views(gout_bf, gout_raw[1], 1))
         gout_words, gout_scales = quantise(gout_bf[:], "gout", Q)
 
-        inv_z = sbt([P, PACK], F32, "inv_z")
-        alpha = sbt([P, PACK], F32, "alpha")
-        gamma = sbt([P, PACK], F32, "gamma")
-        val_words = gather(val_pool[:].bitcast(U32), U32, "val_words")
-        z = sb.tile([P, PACK], F32, name="z", tag="val_pool", align_bytes=64)
+        val_scales = gather(val_bytes[:], U8, "val_scales")
+        z = sbt([P, PACK], F32, "z", after="val_bytes")
         nc.vector.tensor_reduce(z[:], z_parts[:].rearrange("p t r -> p r t"), mybir.AxisListType.X, ALU.add)
+        val_words = gather(val_pool[:].bitcast(U32), U32, "val_words")
+        inv_z = sbt([P, PACK], F32, "inv_z", after="val_pool")
+        inv_z2 = sbt([P, PACK], F32, "inv_z2")
+        alpha = sbt([P, PACK], F32, "alpha")
         nc.vector.reciprocal(inv_z[:], z[:])
-        nc.vector.scalar_tensor_tensor(out=alpha[:], in0=row_vec["qs"][:], scalar=2.0, in1=inv_z[:],
-                                       op0=ALU.mult, op1=ALU.mult)
-        nc.vector.scalar_tensor_tensor(out=gamma[:], in0=alpha[:], scalar=-1.0, in1=inv_z[:],
+        nc.vector.tensor_tensor(inv_z2[:], inv_z[:], inv_z[:], ALU.mult)
+        nc.vector.scalar_tensor_tensor(out=alpha[:], in0=qs_sb[:], scalar=2.0, in1=inv_z[:],
                                        op0=ALU.mult, op1=ALU.mult)
 
         qrows_bf = sbt([P, D * PACK], BF16, "qrows_bf")
@@ -157,7 +180,6 @@ def tile_attend_bsquareshares_k_kernel(tc, query, keys_words, keys_scales, floor
         cast_qrows(0)
 
         weighted = sbt([P, PACK, I], F32, "weighted")
-        total = sbt([P, PACK], F32, "total")
         beta = sbt([P, PACK], F32, "beta")
         slope = sbt([P, PACK, I], F32, "slope")
         for r in range(PACK):
@@ -165,26 +187,21 @@ def tile_attend_bsquareshares_k_kernel(tc, query, keys_words, keys_scales, floor
             nc.tensor.matmul_mx(out=c0[:], lhsT=gout_words[:, P * r:P * r + P].bitcast(FP8X4),
                                 lhsT_scale=gout_scales[:, P * r:P * r + P],
                                 rhs=val_words[:].bitcast(FP8X4), rhs_scale=val_scales[:], start=True, stop=True)
-            nc.vector.scalar_tensor_tensor(out=weighted[:, r, :], in0=squares[:, r, :],
-                                           scalar=row_vec["floor"][:, r:r + 1], in1=c0[:],
-                                           op0=ALU.add, op1=ALU.mult, accum_out=total[:, r:r + 1])
-            nc.scalar.activation(beta[:, r:r + 1], total[:, r:r + 1], ACT.Copy, scale=gamma[:, r:r + 1])
+            nc.vector.scalar_tensor_tensor(out=weighted[:, r, :], in0=c0[:], scalar=inv_z2[:, r:r + 1],
+                                           in1=parts[:, r, :], op0=ALU.mult, op1=ALU.mult,
+                                           accum_out=beta[:, r:r + 1])
             nc.scalar.activation(slope[:, r, :], c0[:], ACT.Identity, bias=beta[:, r:r + 1],
                                  scale=alpha[:, r:r + 1])
 
         qrows_q = [quantise(qrows_bf[:, 0:1024], "qrows0", 256)]
+        cast_qrows(1)
         gs_bf = sbt([P, I * PACK], BF16, "gs_bf")
         for h in range(2):
             nc.vector.tensor_tensor(out=gs_bf[:, 512 * h:512 * h + 512].rearrange("p (i r) -> p i r", r=PACK),
                                     in0=score[h][:].rearrange("p r i -> p i r"),
                                     in1=slope[:, :, P * h:P * h + P].rearrange("p r i -> p i r"), op=ALU.mult)
         gs_words, gs_scales = quantise(gs_bf[:], "gs", I)
-        cast_qrows(1)
-
-        fade_ps = ps.tile([P, P], F32, name="fade_ps", tag="back", bufs=2)
-        nc.tensor.transpose(fade_ps[:], fade_rows[:], ident[:])
-        fade_col = sbt([P, U // P], F32, "fade_col")
-        nc.scalar.copy(fade_col[:], fade_ps[:, 0:U // P])
+        qrows_q.append(quantise(qrows_bf[:, 1024:2048], "qrows1", 256))
 
         faded = [[None] * (U // P) for pair in range(2)]
 
@@ -213,30 +230,33 @@ def tile_attend_bsquareshares_k_kernel(tc, query, keys_words, keys_scales, floor
             return gk
 
         def scatter(j):
-            nc.vector.tensor_copy(windows[j % 2][:].indirect(places[:]), gks[j][:])
+            nc.vector.tensor_copy(windows[j][:].indirect(places[:]), gks[j][:])
 
         def finish(j):
             for half in range(2):
-                bank = ps.tile([P, PACK, P], F32, name="back%d_%d" % (j, half), tag="back" if j < 2 else "wide",
-                               bufs=2 if j < 2 else 4)
+                bank = ps.tile([P, PACK, P], F32, name="back%d_%d" % (j, half), tag="back" if j == 2 else "wide",
+                               bufs=2 if j == 2 else 4)
                 for cc in range(PACK):
                     nc.tensor.transpose(bank[:, cc, :], faded[j // 2][PACK * half + cc][:, P * (j % 2):P * (j % 2) + P],
                                         ident[:])
-                res = sbt([P, 512], F32, "res%d_%d" % (j, half))
+                res = sbt([P, 512], F32, "res%d_%d" % (j, half), after="res0_%d" % half if j == 2 else None)
                 nc.vector.tensor_tensor(out=res[:], in0=bank[:].rearrange("p c n -> p (c n)"),
-                                        in1=windows[j % 2][:, 512 * half:512 * half + 512], op=ALU.add)
+                                        in1=windows[j][:, 512 * half:512 * half + 512], op=ALU.add)
                 nc.sync.dma_start(out=out[P * j:P * j + P, 512 * half:512 * half + 512], in_=res[:])
 
-        gks = [key_grad(0), key_grad(1)]
-        fade_pair(0)
-        scatter(0)
-        qrows_q.append(quantise(qrows_bf[:, 1024:2048], "qrows1", 256))
-        scatter(1)
-        gks.extend([key_grad(2), key_grad(3)])
-        finish(0)
+        gks = [key_grad(j) for j in range(4)]
+        for j in range(4):
+            scatter(j)
+
         fade_pair(1)
-        scatter(2)
-        finish(1)
-        scatter(3)
+        for j in range(2):
+            prod = sbt([P, U], F32, "prod%d" % j, after="qrows_bf")
+            nc.gpsimd.tensor_tensor(prod[:], old_sb[j][:], fade_all[:], ALU.mult)
+            for half in range(2):
+                cols = slice(512 * half, 512 * half + 512)
+                res = sbt([P, 512], F32, "res%d_%d" % (j, half))
+                nc.gpsimd.tensor_tensor(res[:], prod[:, cols], windows[j][:, cols], ALU.add)
+                queue = nc.sync if j == 0 else nc.scalar
+                queue.dma_start(out=out[P * j:P * j + P, cols], in_=res[:])
         finish(2)
         finish(3)

@@ -37,8 +37,6 @@ def tile_attend_bsquareshares_k_kernel(tc, query, keys_words, keys_scales, floor
         val_bytes = sbt([P, T], U8, "val_bytes")
         nc.gpsimd.memset(key_bytes[:].bitcast(I32), 0)
         nc.gpsimd.memset(val_bytes[:].bitcast(I32), 0)
-        fade_rows = sbt([P, P], F32, "fade_rows")
-        nc.gpsimd.memset(fade_rows[:], 0.0)
 
         def load_words(pool_tile, words):
             nc.sync.dma_start(out=pool_tile[:], in_=words[0].rearrange("p n t -> p (n t)").bitcast(I32))
@@ -58,35 +56,34 @@ def tile_attend_bsquareshares_k_kernel(tc, query, keys_words, keys_scales, floor
         load_bytes(key_bytes, keys_scales)
         query_raw.append(load_half(query, "query", 1))
         load_words(key_pool, keys_words)
-        gout_raw = [load_half(gout, "gout", h) for h in range(2)]
-        load_words(val_pool, vals_words)
+        gout_raw = [load_half(gout, "gout", 0)]
         load_bytes(val_bytes, vals_scales)
+        gout_raw.append(load_half(gout, "gout", 1))
+        load_words(val_pool, vals_words)
 
         def load_rows(queue, src, name):
             v = sbt([P, PACK], F32, name)
             queue.dma_start(out=v[:], in_=src.rearrange("(p r) o -> p (r o)", r=PACK))
             return v
 
-        qs_sb = load_rows(nc.sync, qs, "qs_sb")
         qrows_raw = [load_half(qrows, "qrows", h) for h in range(2)]
+        nc.sync.dma_start(places[:], offs4)
+        fade_all = sbt([P, U], F32, "fade_all")
+        nc.sync.dma_start(out=fade_all[:], in_=fade[0].partition_broadcast(P))
         old_sb = []
         for j in range(4):
             o = sbt([P, U], F32, "old%d" % j)
             nc.sync.dma_start(out=o[:], in_=old[P * j:P * j + P, :])
             old_sb.append(o)
-            if j == 1:
-                nc.sync.dma_start(places[:], offs4)
 
-        nc.gpsimd.dma_start(out=fade_rows[0:U // P, :], in_=fade.rearrange("o (c n) -> (o c) n", n=P))
-        ident = sbt([P, P], F32, "ident")
-        make_identity(nc, ident[:])
         floor_sb = load_rows(nc.gpsimd, floor, "floor_sb")
+        qs_sb = load_rows(nc.gpsimd, qs, "qs_sb")
         reserve_sb = load_rows(nc.gpsimd, reserve, "reserve_sb")
 
         windows = []
         for j in range(4):
             w = sbt([P, U], F32, "window%d" % j)
-            nc.vector.memset(w[:], 0.0)
+            nc.vector.memset(w[:].bitcast(I32), 0)
             windows.append(w)
 
         def gather(window, dtype, name, after=None):
@@ -99,8 +96,8 @@ def tile_attend_bsquareshares_k_kernel(tc, query, keys_words, keys_scales, floor
             src = raw[:].rearrange("p j (s r) -> p s r j", r=PACK)
             return dst, src
 
-        def quantise(bf, name, width):
-            words = sbt([P, width], U32, name + "_words")
+        def quantise(bf, name, width, after=None):
+            words = sbt([P, width], U32, name + "_words", after)
             scales = sbt([P, width], U8, name + "_scales")
             nc.vector.quantize_mx(out=words[:].bitcast(FP8X4), scales=scales[:], in_=bf)
             return words, scales
@@ -133,19 +130,6 @@ def tile_attend_bsquareshares_k_kernel(tc, query, keys_words, keys_scales, floor
                 nc.scalar.activation(squares[:, r, P * h:P * h + P], score[h][:, r, :], ACT.Square,
                                      accum_out=z_parts[:, h, r:r + 1])
 
-        fade_ps = ps.tile([P, P], F32, name="fade_ps", tag="back", bufs=2)
-        nc.tensor.transpose(fade_ps[:], fade_rows[:], ident[:])
-        fade_col = sbt([P, U // P], F32, "fade_col", after="key_words")
-        nc.scalar.copy(fade_col[:], fade_ps[:, 0:U // P])
-
-        fade_all = sbt([P, U], F32, "fade_all")
-        for half in range(2):
-            bank = ps.tile([P, PACK, P], F32, name="spread%d" % half, tag="back", bufs=2)
-            for cc in range(PACK):
-                c = PACK * half + cc
-                nc.tensor.transpose(bank[:, cc, :], fade_col[:, c:c + 1].to_broadcast([P, P]), ident[:])
-            nc.scalar.copy(fade_all[:, 512 * half:512 * half + 512], bank[:].rearrange("p c n -> p (c n)"))
-
         minus_two_qs = sbt([P, PACK], F32, "minus_two_qs")
         nc.gpsimd.tensor_scalar(minus_two_qs[:], qs_sb[:], -2.0, 0.0, ALU.mult, ALU.add)
         parts = sbt([P, PACK, I], F32, "parts")
@@ -153,16 +137,22 @@ def tile_attend_bsquareshares_k_kernel(tc, query, keys_words, keys_scales, floor
             nc.gpsimd.tensor_scalar(parts[:, r, :], squares[:, r, :], floor_sb[:, r:r + 1], minus_two_qs[:, r:r + 1],
                                     ALU.add, ALU.mult)
 
+        fade_rows = sbt([P, P], F32, "fade_rows")
+        nc.gpsimd.memset(fade_rows[:], 0.0)
+        nc.gpsimd.dma_start(out=fade_rows[0:U // P, :], in_=fade.rearrange("o (c n) -> (o c) n", n=P))
+        ident = sbt([P, P], F32, "ident")
+        make_identity(nc, ident[:])
+
         gout_bf = sbt([P, Q * PACK], BF16, "gout_bf", after="key_pool")
         nc.vector.tensor_copy(*dealt_views(gout_bf, gout_raw[0], 0))
+        val_scales = gather(val_bytes[:], U8, "val_scales", after="gout_raw0")
         nc.vector.tensor_copy(*dealt_views(gout_bf, gout_raw[1], 1))
         gout_words, gout_scales = quantise(gout_bf[:], "gout", Q)
 
-        val_scales = gather(val_bytes[:], U8, "val_scales")
-        z = sbt([P, PACK], F32, "z", after="val_bytes")
-        nc.vector.tensor_reduce(z[:], z_parts[:].rearrange("p t r -> p r t"), mybir.AxisListType.X, ALU.add)
         val_words = gather(val_pool[:].bitcast(U32), U32, "val_words")
-        inv_z = sbt([P, PACK], F32, "inv_z", after="val_pool")
+        z = sbt([P, PACK], F32, "z", after="val_pool")
+        nc.vector.tensor_reduce(z[:], z_parts[:].rearrange("p t r -> p r t"), mybir.AxisListType.X, ALU.add)
+        inv_z = sbt([P, PACK], F32, "inv_z")
         inv_z2 = sbt([P, PACK], F32, "inv_z2")
         alpha = sbt([P, PACK], F32, "alpha")
         nc.vector.reciprocal(inv_z[:], z[:])
@@ -200,24 +190,17 @@ def tile_attend_bsquareshares_k_kernel(tc, query, keys_words, keys_scales, floor
             nc.vector.tensor_tensor(out=gs_bf[:, 512 * h:512 * h + 512].rearrange("p (i r) -> p i r", r=PACK),
                                     in0=score[h][:].rearrange("p r i -> p i r"),
                                     in1=slope[:, :, P * h:P * h + P].rearrange("p r i -> p i r"), op=ALU.mult)
-        gs_words, gs_scales = quantise(gs_bf[:], "gs", I)
-        qrows_q.append(quantise(qrows_bf[:, 1024:2048], "qrows1", 256))
+        gs_words = sbt([P, I], U32, "gs_words")
+        gs_scales = sbt([P, I], U8, "gs_scales")
+        for h in range(2):
+            nc.vector.quantize_mx(out=gs_words[:, P * h:P * h + P].bitcast(FP8X4), scales=gs_scales[:, P * h:P * h + P],
+                                  in_=gs_bf[:, 512 * h:512 * h + 512])
+        qrows_q.append(quantise(qrows_bf[:, 1024:2048], "qrows1", 256, after="gs_bf"))
 
-        faded = [[None] * (U // P) for pair in range(2)]
-
-        def fade_pair(pair):
-            for c2 in range(U // P // 2):
-                bank = ps.tile([P, 2, 2, P], F32, name="turn%d_%d" % (pair, c2), tag="wide", bufs=4)
-                for cc in range(2):
-                    c = 2 * c2 + cc
-                    for jj in range(2):
-                        nc.tensor.transpose(bank[:, cc, jj, :], old_sb[2 * pair + jj][:, P * c:P * c + P], ident[:])
-                for cc in range(2):
-                    c = 2 * c2 + cc
-                    f = sbt([P, 2 * P], F32, "faded%d_%d" % (pair, c))
-                    nc.scalar.activation(f[:], bank[:, cc, :, :].rearrange("p j d -> p (j d)"), ACT.Copy,
-                                         scale=fade_col[:, c:c + 1])
-                    faded[pair][c] = f
+        fade_ps = ps.tile([P, P], F32, name="fade_ps", tag="wide", bufs=4)
+        nc.tensor.transpose(fade_ps[:], fade_rows[:], ident[:])
+        fade_col = sbt([P, U // P], F32, "fade_col")
+        nc.scalar.copy(fade_col[:], fade_ps[:, 0:U // P])
 
         def key_grad(j):
             words, scales = qrows_q[j // 2]
@@ -232,31 +215,39 @@ def tile_attend_bsquareshares_k_kernel(tc, query, keys_words, keys_scales, floor
         def scatter(j):
             nc.vector.tensor_copy(windows[j][:].indirect(places[:]), gks[j][:])
 
-        def finish(j):
-            for half in range(2):
-                bank = ps.tile([P, PACK, P], F32, name="back%d_%d" % (j, half), tag="back" if j == 2 else "wide",
-                               bufs=2 if j == 2 else 4)
-                for cc in range(PACK):
-                    nc.tensor.transpose(bank[:, cc, :], faded[j // 2][PACK * half + cc][:, P * (j % 2):P * (j % 2) + P],
-                                        ident[:])
-                res = sbt([P, 512], F32, "res%d_%d" % (j, half), after="res0_%d" % half if j == 2 else None)
-                nc.vector.tensor_tensor(out=res[:], in0=bank[:].rearrange("p c n -> p (c n)"),
-                                        in1=windows[j][:, 512 * half:512 * half + 512], op=ALU.add)
-                nc.sync.dma_start(out=out[P * j:P * j + P, 512 * half:512 * half + 512], in_=res[:])
+        def store(queue, j, half, res):
+            queue.dma_start(out=out[P * j:P * j + P, 512 * half:512 * half + 512], in_=res[:])
 
         gks = [key_grad(j) for j in range(4)]
         for j in range(4):
             scatter(j)
 
-        fade_pair(1)
-        for j in range(2):
-            prod = sbt([P, U], F32, "prod%d" % j, after="qrows_bf")
-            nc.gpsimd.tensor_tensor(prod[:], old_sb[j][:], fade_all[:], ALU.mult)
-            for half in range(2):
+        turned_halves = [(2, 0), (3, 0), (1, 1), (2, 1), (3, 1)]
+        faded = {}
+        for c in range(U // P):
+            tiles = [j for j, half in turned_halves if half == c // PACK]
+            bank = ps.tile([P, len(tiles), P], F32, name="turn%d" % c, tag="wide", bufs=4)
+            for n, j in enumerate(tiles):
+                nc.tensor.transpose(bank[:, n, :], old_sb[j][:, P * c:P * c + P], ident[:])
+            f = sbt([P, len(tiles), P], F32, "faded%d" % c)
+            nc.scalar.activation(f[:], bank[:], ACT.Copy, scale=fade_col[:, c:c + 1])
+            for n, j in enumerate(tiles):
+                faded[j, c] = f[:, n, :]
+
+        for j, width in ((0, U), (1, 512)):
+            prod = sbt([P, width], F32, "prod%d" % j, after="qrows_bf")
+            nc.gpsimd.tensor_tensor(prod[:], old_sb[j][:, 0:width], fade_all[:, 0:width], ALU.mult)
+            for half in range(width // 512):
                 cols = slice(512 * half, 512 * half + 512)
                 res = sbt([P, 512], F32, "res%d_%d" % (j, half))
                 nc.gpsimd.tensor_tensor(res[:], prod[:, cols], windows[j][:, cols], ALU.add)
-                queue = nc.sync if j == 0 else nc.scalar
-                queue.dma_start(out=out[P * j:P * j + P, cols], in_=res[:])
-        finish(2)
-        finish(3)
+                store(nc.sync if j == 0 else nc.scalar, j, half, res)
+
+        for n, (j, half) in enumerate(turned_halves):
+            bank = ps.tile([P, PACK, P], F32, name="back%d" % n, tag="back" if n < 2 else "wide", bufs=2 if n < 2 else 4)
+            for cc in range(PACK):
+                nc.tensor.transpose(bank[:, cc, :], faded[j, PACK * half + cc], ident[:])
+            res = sbt([P, 512], F32, "res%d_%d" % (j, half), after="res0_0" if n == 0 else None)
+            nc.vector.tensor_tensor(out=res[:], in0=bank[:].rearrange("p c n -> p (c n)"),
+                                    in1=windows[j][:, 512 * half:512 * half + 512], op=ALU.add)
+            store(nc.sync, j, half, res)

@@ -16,6 +16,12 @@ ACT = mybir.ActivationFunctionType
 D, E, T, I, Q, U = 512, 512, 1024, 256, 512, 1024
 P = 128
 PACK = 4
+HALF_COLS = 256
+BANK = 512
+TILES = D // P
+CHUNKS = U // P
+GPSIMD_COLS = ((0, U), (1, BANK))
+TURNED = ((2, 0), (3, 0), (1, 1), (2, 1), (3, 1))
 FLOPS = 2 * Q * I * (D + E + D)
 
 
@@ -28,6 +34,15 @@ def tile_attend_bsquareshares_k_kernel(tc, query, keys_words, keys_scales, floor
 
         def sbt(shape, dtype, name, after=None):
             return sb.tile(shape, dtype, name=name, tag=after or name, align_bytes=64)
+
+        def score_bank(shape, name):
+            return ps.tile(shape, F32, name=name, tag="score", bufs=2)
+
+        def wide_bank(shape, name):
+            return ps.tile(shape, F32, name=name, tag="wide", bufs=4)
+
+        def back_bank(shape, name):
+            return ps.tile(shape, F32, name=name, tag="back", bufs=2)
 
         slots = sbt([P, I // 16], U16, "slots")
         places = sbt([P, I // 16], U16, "places")
@@ -47,9 +62,15 @@ def tile_attend_bsquareshares_k_kernel(tc, query, keys_words, keys_scales, floor
                                   in_=scales[0, 4 * quad:4 * quad + 4, :].bitcast(I32))
 
         def load_half(src, name, h):
-            raw = sbt([P, PACK, 256], F32, "%s_raw%d" % (name, h))
-            nc.sync.dma_start(out=raw[:], in_=src.rearrange("(p j) c -> p j c", j=PACK)[:, :, 256 * h:256 * h + 256])
+            raw = sbt([P, PACK, HALF_COLS], F32, "%s_raw%d" % (name, h))
+            rows = src.rearrange("(p j) c -> p j c", j=PACK)
+            nc.sync.dma_start(out=raw[:], in_=rows[:, :, HALF_COLS * h:HALF_COLS * (h + 1)])
             return raw
+
+        def load_rows(src, name):
+            v = sbt([P, PACK], F32, name)
+            nc.gpsimd.dma_start(out=v[:], in_=src.rearrange("(p r) o -> p (r o)", r=PACK))
+            return v
 
         nc.sync.dma_start(slots[:], offs)
         query_raw = [load_half(query, "query", 0)]
@@ -60,28 +81,22 @@ def tile_attend_bsquareshares_k_kernel(tc, query, keys_words, keys_scales, floor
         load_bytes(val_bytes, vals_scales)
         gout_raw.append(load_half(gout, "gout", 1))
         load_words(val_pool, vals_words)
-
-        def load_rows(queue, src, name):
-            v = sbt([P, PACK], F32, name)
-            queue.dma_start(out=v[:], in_=src.rearrange("(p r) o -> p (r o)", r=PACK))
-            return v
-
         qrows_raw = [load_half(qrows, "qrows", h) for h in range(2)]
         nc.sync.dma_start(places[:], offs4)
         fade_all = sbt([P, U], F32, "fade_all")
         nc.sync.dma_start(out=fade_all[:], in_=fade[0].partition_broadcast(P))
         old_sb = []
-        for j in range(4):
+        for j in range(TILES):
             o = sbt([P, U], F32, "old%d" % j)
             nc.sync.dma_start(out=o[:], in_=old[P * j:P * j + P, :])
             old_sb.append(o)
 
-        floor_sb = load_rows(nc.gpsimd, floor, "floor_sb")
-        qs_sb = load_rows(nc.gpsimd, qs, "qs_sb")
-        reserve_sb = load_rows(nc.gpsimd, reserve, "reserve_sb")
+        floor_sb = load_rows(floor, "floor_sb")
+        qs_sb = load_rows(qs, "qs_sb")
+        reserve_sb = load_rows(reserve, "reserve_sb")
 
         windows = []
-        for j in range(4):
+        for j in range(TILES):
             w = sbt([P, U], F32, "window%d" % j)
             nc.vector.memset(w[:].bitcast(I32), 0)
             windows.append(w)
@@ -92,7 +107,8 @@ def tile_attend_bsquareshares_k_kernel(tc, query, keys_words, keys_scales, floor
             return picked
 
         def dealt_views(bf, raw, h):
-            dst = bf[:].rearrange("p (r s j) -> p s r j", r=PACK, j=PACK)[:, 64 * h:64 * h + 64, :, :]
+            s_half = HALF_COLS // PACK
+            dst = bf[:].rearrange("p (r s j) -> p s r j", r=PACK, j=PACK)[:, s_half * h:s_half * (h + 1), :, :]
             src = raw[:].rearrange("p j (s r) -> p s r j", r=PACK)
             return dst, src
 
@@ -111,7 +127,7 @@ def tile_attend_bsquareshares_k_kernel(tc, query, keys_words, keys_scales, floor
 
         score = []
         for h in range(2):
-            bank = ps.tile([P, PACK, P], F32, name="score%d" % h, tag="score", bufs=2)
+            bank = score_bank([P, PACK, P], "score%d" % h)
             for r in range(PACK):
                 nc.tensor.matmul_mx(out=bank[:, r, :],
                                     lhsT=query_words[:, P * r:P * r + P].bitcast(FP8X4),
@@ -120,15 +136,15 @@ def tile_attend_bsquareshares_k_kernel(tc, query, keys_words, keys_scales, floor
                                     rhs_scale=key_scales[:, P * h:P * h + P], start=True, stop=True)
             score.append(bank)
 
-        z_parts = sbt([P, 3, PACK], F32, "z_parts")
+        z_terms = sbt([P, 3, PACK], F32, "z_terms")
         floors = sbt([P, PACK], F32, "floors")
         nc.gpsimd.tensor_scalar(floors[:], floor_sb[:], float(I), 0.0, ALU.mult, ALU.add)
-        nc.gpsimd.tensor_tensor(z_parts[:, 2, :], floors[:], reserve_sb[:], ALU.add)
+        nc.gpsimd.tensor_tensor(z_terms[:, 2, :], floors[:], reserve_sb[:], ALU.add)
         squares = sbt([P, PACK, I], F32, "squares")
         for h in range(2):
             for r in range(PACK):
                 nc.scalar.activation(squares[:, r, P * h:P * h + P], score[h][:, r, :], ACT.Square,
-                                     accum_out=z_parts[:, h, r:r + 1])
+                                     accum_out=z_terms[:, h, r:r + 1])
 
         minus_two_qs = sbt([P, PACK], F32, "minus_two_qs")
         nc.gpsimd.tensor_scalar(minus_two_qs[:], qs_sb[:], -2.0, 0.0, ALU.mult, ALU.add)
@@ -139,7 +155,7 @@ def tile_attend_bsquareshares_k_kernel(tc, query, keys_words, keys_scales, floor
 
         fade_rows = sbt([P, P], F32, "fade_rows")
         nc.gpsimd.memset(fade_rows[:], 0.0)
-        nc.gpsimd.dma_start(out=fade_rows[0:U // P, :], in_=fade.rearrange("o (c n) -> (o c) n", n=P))
+        nc.gpsimd.dma_start(out=fade_rows[0:CHUNKS, :], in_=fade.rearrange("o (c n) -> (o c) n", n=P))
         ident = sbt([P, P], F32, "ident")
         make_identity(nc, ident[:])
 
@@ -151,7 +167,7 @@ def tile_attend_bsquareshares_k_kernel(tc, query, keys_words, keys_scales, floor
 
         val_words = gather(val_pool[:].bitcast(U32), U32, "val_words")
         z = sbt([P, PACK], F32, "z", after="val_pool")
-        nc.vector.tensor_reduce(z[:], z_parts[:].rearrange("p t r -> p r t"), mybir.AxisListType.X, ALU.add)
+        nc.vector.tensor_reduce(z[:], z_terms[:].rearrange("p t r -> p r t"), mybir.AxisListType.X, ALU.add)
         inv_z = sbt([P, PACK], F32, "inv_z")
         inv_z2 = sbt([P, PACK], F32, "inv_z2")
         alpha = sbt([P, PACK], F32, "alpha")
@@ -161,9 +177,10 @@ def tile_attend_bsquareshares_k_kernel(tc, query, keys_words, keys_scales, floor
                                        op0=ALU.mult, op1=ALU.mult)
 
         qrows_bf = sbt([P, D * PACK], BF16, "qrows_bf")
+        half_bf = HALF_COLS * PACK
 
         def cast_qrows(h):
-            dst = qrows_bf[:, 1024 * h:1024 * h + 1024].rearrange("p (c i t) -> p c t i", i=4, t=PACK)
+            dst = qrows_bf[:, half_bf * h:half_bf * (h + 1)].rearrange("p (c i t) -> p c t i", i=4, t=PACK)
             src = qrows_raw[h][:].rearrange("p t (c i) -> p c t i", i=4)
             nc.scalar.copy(dst, src)
 
@@ -173,7 +190,7 @@ def tile_attend_bsquareshares_k_kernel(tc, query, keys_words, keys_scales, floor
         beta = sbt([P, PACK], F32, "beta")
         slope = sbt([P, PACK, I], F32, "slope")
         for r in range(PACK):
-            c0 = ps.tile([P, I], F32, name="c0_%d" % r, tag="wide", bufs=4)
+            c0 = wide_bank([P, I], "c0_%d" % r)
             nc.tensor.matmul_mx(out=c0[:], lhsT=gout_words[:, P * r:P * r + P].bitcast(FP8X4),
                                 lhsT_scale=gout_scales[:, P * r:P * r + P],
                                 rhs=val_words[:].bitcast(FP8X4), rhs_scale=val_scales[:], start=True, stop=True)
@@ -183,50 +200,45 @@ def tile_attend_bsquareshares_k_kernel(tc, query, keys_words, keys_scales, floor
             nc.scalar.activation(slope[:, r, :], c0[:], ACT.Identity, bias=beta[:, r:r + 1],
                                  scale=alpha[:, r:r + 1])
 
-        qrows_q = [quantise(qrows_bf[:, 0:1024], "qrows0", 256)]
+        qrows_q = [quantise(qrows_bf[:, 0:half_bf], "qrows0", HALF_COLS)]
         cast_qrows(1)
         gs_bf = sbt([P, I * PACK], BF16, "gs_bf")
         for h in range(2):
-            nc.vector.tensor_tensor(out=gs_bf[:, 512 * h:512 * h + 512].rearrange("p (i r) -> p i r", r=PACK),
+            nc.vector.tensor_tensor(out=gs_bf[:, BANK * h:BANK * (h + 1)].rearrange("p (i r) -> p i r", r=PACK),
                                     in0=score[h][:].rearrange("p r i -> p i r"),
                                     in1=slope[:, :, P * h:P * h + P].rearrange("p r i -> p i r"), op=ALU.mult)
         gs_words = sbt([P, I], U32, "gs_words")
         gs_scales = sbt([P, I], U8, "gs_scales")
         for h in range(2):
             nc.vector.quantize_mx(out=gs_words[:, P * h:P * h + P].bitcast(FP8X4), scales=gs_scales[:, P * h:P * h + P],
-                                  in_=gs_bf[:, 512 * h:512 * h + 512])
-        qrows_q.append(quantise(qrows_bf[:, 1024:2048], "qrows1", 256, after="gs_bf"))
+                                  in_=gs_bf[:, BANK * h:BANK * (h + 1)])
+        qrows_q.append(quantise(qrows_bf[:, half_bf:2 * half_bf], "qrows1", HALF_COLS, after="gs_bf"))
 
-        fade_ps = ps.tile([P, P], F32, name="fade_ps", tag="wide", bufs=4)
+        fade_ps = wide_bank([P, P], "fade_ps")
         nc.tensor.transpose(fade_ps[:], fade_rows[:], ident[:])
-        fade_col = sbt([P, U // P], F32, "fade_col")
-        nc.scalar.copy(fade_col[:], fade_ps[:, 0:U // P])
+        fade_col = sbt([P, CHUNKS], F32, "fade_col")
+        nc.scalar.copy(fade_col[:], fade_ps[:, 0:CHUNKS])
 
-        def key_grad(j):
+        gks = []
+        for j in range(TILES):
             words, scales = qrows_q[j // 2]
             cols = slice(P * (j % 2), P * (j % 2) + P)
-            bank = ps.tile([P, I], F32, name="gk_ps%d" % j, tag="score", bufs=2)
+            bank = score_bank([P, I], "gk_ps%d" % j)
             nc.tensor.matmul_mx(out=bank[:], lhsT=words[:, cols].bitcast(FP8X4), lhsT_scale=scales[:, cols],
                                 rhs=gs_words[:].bitcast(FP8X4), rhs_scale=gs_scales[:], start=True, stop=True)
             gk = sbt([P, I], F32, "gk%d" % j)
             nc.scalar.copy(gk[:], bank[:])
-            return gk
-
-        def scatter(j):
+            gks.append(gk)
+        for j in range(TILES):
             nc.vector.tensor_copy(windows[j][:].indirect(places[:]), gks[j][:])
 
         def store(queue, j, half, res):
-            queue.dma_start(out=out[P * j:P * j + P, 512 * half:512 * half + 512], in_=res[:])
+            queue.dma_start(out=out[P * j:P * j + P, BANK * half:BANK * (half + 1)], in_=res[:])
 
-        gks = [key_grad(j) for j in range(4)]
-        for j in range(4):
-            scatter(j)
-
-        turned_halves = [(2, 0), (3, 0), (1, 1), (2, 1), (3, 1)]
         faded = {}
-        for c in range(U // P):
-            tiles = [j for j, half in turned_halves if half == c // PACK]
-            bank = ps.tile([P, len(tiles), P], F32, name="turn%d" % c, tag="wide", bufs=4)
+        for c in range(CHUNKS):
+            tiles = [j for j, half in TURNED if half == c // PACK]
+            bank = wide_bank([P, len(tiles), P], "turn%d" % c)
             for n, j in enumerate(tiles):
                 nc.tensor.transpose(bank[:, n, :], old_sb[j][:, P * c:P * c + P], ident[:])
             f = sbt([P, len(tiles), P], F32, "faded%d" % c)
@@ -234,20 +246,24 @@ def tile_attend_bsquareshares_k_kernel(tc, query, keys_words, keys_scales, floor
             for n, j in enumerate(tiles):
                 faded[j, c] = f[:, n, :]
 
-        for j, width in ((0, U), (1, 512)):
-            prod = sbt([P, width], F32, "prod%d" % j, after="qrows_bf")
+        def gpsimd_share(j, width, queue, prod_after, res_after):
+            prod = sbt([P, width], F32, "prod%d" % j, prod_after)
             nc.gpsimd.tensor_tensor(prod[:], old_sb[j][:, 0:width], fade_all[:, 0:width], ALU.mult)
-            for half in range(width // 512):
-                cols = slice(512 * half, 512 * half + 512)
-                res = sbt([P, 512], F32, "res%d_%d" % (j, half))
+            for half in range(width // BANK):
+                cols = slice(BANK * half, BANK * (half + 1))
+                res = sbt([P, BANK], F32, "res%d_%d" % (j, half), res_after)
                 nc.gpsimd.tensor_tensor(res[:], prod[:, cols], windows[j][:, cols], ALU.add)
-                store(nc.sync if j == 0 else nc.scalar, j, half, res)
+                store(queue, j, half, res)
 
-        for n, (j, half) in enumerate(turned_halves):
-            bank = ps.tile([P, PACK, P], F32, name="back%d" % n, tag="back" if n < 2 else "wide", bufs=2 if n < 2 else 4)
+        gpsimd_share(*GPSIMD_COLS[0], nc.sync, "qrows_bf", None)
+
+        for n, (j, half) in enumerate(TURNED):
+            bank = (back_bank if n < 2 else wide_bank)([P, PACK, P], "back%d" % n)
             for cc in range(PACK):
                 nc.tensor.transpose(bank[:, cc, :], faded[j, PACK * half + cc], ident[:])
-            res = sbt([P, 512], F32, "res%d_%d" % (j, half), after="res0_0" if n == 0 else None)
+            res = sbt([P, BANK], F32, "res%d_%d" % (j, half), after="qrows_bf" if n == 0 else None)
             nc.vector.tensor_tensor(out=res[:], in0=bank[:].rearrange("p c n -> p (c n)"),
-                                    in1=windows[j][:, 512 * half:512 * half + 512], op=ALU.add)
+                                    in1=windows[j][:, BANK * half:BANK * (half + 1)], op=ALU.add)
             store(nc.sync, j, half, res)
+
+        gpsimd_share(*GPSIMD_COLS[1], nc.scalar, "old0", "faded%d" % (CHUNKS - 1))

from contextlib import ExitStack

import concourse.mybir as mybir
from concourse.masks import make_identity

F32 = mybir.dt.float32
BF16 = mybir.dt.bfloat16
I32 = mybir.dt.int32
U32 = mybir.dt.uint32
U16 = mybir.dt.uint16
U8 = mybir.dt.uint8
FP8X4 = mybir.dt.float8_e4m3fn_x4
ALU = mybir.AluOpType
ACT = mybir.ActivationFunctionType

D, E, T, I, Q, U = 512, 512, 1024, 256, 512, 1024
P = 128
PACK = 4
HALF_COLS = 256
BANK = 512
TILES = D // P
CHUNKS = U // P
GPSIMD_COLS = ((0, U), (1, BANK))
TURNED = ((2, 0), (3, 0), (1, 1), (2, 1), (3, 1))
FLOPS = 2 * Q * I * (D + E + D)


def tile_attend_bsquareshares_k_kernel(tc, query, keys_words, keys_scales, floor, reserve, gout,
                                        vals_words, vals_scales, qs, qrows, old, fade, offs, offs4, out):
    nc = tc.nc
    with ExitStack() as ctx:
        sb = ctx.enter_context(tc.tile_pool(name="sb", bufs=1))
        ps = ctx.enter_context(tc.psum_pool(name="ps", bufs=1))

        def sbt(shape, dtype, name, after=None):
            return sb.tile(shape, dtype, name=name, tag=after or name, align_bytes=64)

        def score_bank(shape, name):
            return ps.tile(shape, F32, name=name, tag="score", bufs=2)

        def wide_bank(shape, name):
            return ps.tile(shape, F32, name=name, tag="wide", bufs=4)

        def back_bank(shape, name):
            return ps.tile(shape, F32, name=name, tag="back", bufs=2)

        slots = sbt([P, I // 16], U16, "slots")
        places = sbt([P, I // 16], U16, "places")
        key_pool = sbt([P, T], I32, "key_pool")
        val_pool = sbt([P, T], I32, "val_pool")
        key_bytes = sbt([P, T], U8, "key_bytes")
        val_bytes = sbt([P, T], U8, "val_bytes")
        nc.gpsimd.memset(key_bytes[:].bitcast(I32), 0)
        nc.gpsimd.memset(val_bytes[:].bitcast(I32), 0)

        def load_words(pool_tile, words):
            nc.sync.dma_start(out=pool_tile[:], in_=words[0].rearrange("p n t -> p (n t)").bitcast(I32))

        def load_bytes(byte_tile, scales):
            for quad in range(4):
                nc.sync.dma_start(out=byte_tile[32 * quad:32 * quad + 4, :].bitcast(I32),
                                  in_=scales[0, 4 * quad:4 * quad + 4, :].bitcast(I32))

        def load_half(src, name, h):
            raw = sbt([P, PACK, HALF_COLS], F32, "%s_raw%d" % (name, h))
            rows = src.rearrange("(p j) c -> p j c", j=PACK)
            nc.sync.dma_start(out=raw[:], in_=rows[:, :, HALF_COLS * h:HALF_COLS * (h + 1)])
            return raw

        def load_rows(src, name):
            v = sbt([P, PACK], F32, name)
            nc.gpsimd.dma_start(out=v[:], in_=src.rearrange("(p r) o -> p (r o)", r=PACK))
            return v

        nc.sync.dma_start(slots[:], offs)
        query_raw = [load_half(query, "query", 0)]
        load_bytes(key_bytes, keys_scales)
        query_raw.append(load_half(query, "query", 1))
        load_words(key_pool, keys_words)
        gout_raw = [load_half(gout, "gout", 0)]
        load_bytes(val_bytes, vals_scales)
        gout_raw.append(load_half(gout, "gout", 1))
        load_words(val_pool, vals_words)
        qrows_raw = [load_half(qrows, "qrows", h) for h in range(2)]
        nc.sync.dma_start(places[:], offs4)
        fade_all = sbt([P, U], F32, "fade_all")
        nc.sync.dma_start(out=fade_all[:], in_=fade[0].partition_broadcast(P))
        old_sb = []
        for j in range(TILES):
            o = sbt([P, U], F32, "old%d" % j)
            nc.sync.dma_start(out=o[:], in_=old[P * j:P * j + P, :])
            old_sb.append(o)

        floor_sb = load_rows(floor, "floor_sb")
        qs_sb = load_rows(qs, "qs_sb")
        reserve_sb = load_rows(reserve, "reserve_sb")

        windows = []
        for j in range(TILES):
            w = sbt([P, U], F32, "window%d" % j)
            nc.vector.memset(w[:].bitcast(I32), 0)
            windows.append(w)

        def gather(window, dtype, name, after=None):
            picked = sbt([P, I], dtype, name, after)
            nc.vector.tensor_copy(picked[:], window.indirect(slots[:]))
            return picked

        def dealt_views(bf, raw, h):
            s_half = HALF_COLS // PACK
            dst = bf[:].rearrange("p (r s j) -> p s r j", r=PACK, j=PACK)[:, s_half * h:s_half * (h + 1), :, :]
            src = raw[:].rearrange("p j (s r) -> p s r j", r=PACK)
            return dst, src

        def quantise(bf, name, width, after=None):
            words = sbt([P, width], U32, name + "_words", after)
            scales = sbt([P, width], U8, name + "_scales")
            nc.vector.quantize_mx(out=words[:].bitcast(FP8X4), scales=scales[:], in_=bf)
            return words, scales

        key_scales = gather(key_bytes[:], U8, "key_scales")
        query_bf = sbt([P, Q * PACK], BF16, "query_bf")
        nc.scalar.copy(*dealt_views(query_bf, query_raw[0], 0))
        nc.vector.tensor_copy(*dealt_views(query_bf, query_raw[1], 1))
        query_words, query_scales = quantise(query_bf[:], "query", Q)
        key_words = gather(key_pool[:].bitcast(U32), U32, "key_words")

        score = []
        for h in range(2):
            bank = score_bank([P, PACK, P], "score%d" % h)
            for r in range(PACK):
                nc.tensor.matmul_mx(out=bank[:, r, :],
                                    lhsT=query_words[:, P * r:P * r + P].bitcast(FP8X4),
                                    lhsT_scale=query_scales[:, P * r:P * r + P],
                                    rhs=key_words[:, P * h:P * h + P].bitcast(FP8X4),
                                    rhs_scale=key_scales[:, P * h:P * h + P], start=True, stop=True)
            score.append(bank)

        z_terms = sbt([P, 3, PACK], F32, "z_terms")
        floors = sbt([P, PACK], F32, "floors")
        nc.gpsimd.tensor_scalar(floors[:], floor_sb[:], float(I), 0.0, ALU.mult, ALU.add)
        nc.gpsimd.tensor_tensor(z_terms[:, 2, :], floors[:], reserve_sb[:], ALU.add)
        squares = sbt([P, PACK, I], F32, "squares")
        for h in range(2):
            for r in range(PACK):
                nc.scalar.activation(squares[:, r, P * h:P * h + P], score[h][:, r, :], ACT.Square,
                                     accum_out=z_terms[:, h, r:r + 1])

        minus_two_qs = sbt([P, PACK], F32, "minus_two_qs")
        nc.gpsimd.tensor_scalar(minus_two_qs[:], qs_sb[:], -2.0, 0.0, ALU.mult, ALU.add)
        parts = sbt([P, PACK, I], F32, "parts")
        for r in range(PACK):
            nc.gpsimd.tensor_scalar(parts[:, r, :], squares[:, r, :], floor_sb[:, r:r + 1], minus_two_qs[:, r:r + 1],
                                    ALU.add, ALU.mult)

        fade_rows = sbt([P, P], F32, "fade_rows")
        nc.gpsimd.memset(fade_rows[:], 0.0)
        nc.gpsimd.dma_start(out=fade_rows[0:CHUNKS, :], in_=fade.rearrange("o (c n) -> (o c) n", n=P))
        ident = sbt([P, P], F32, "ident")
        make_identity(nc, ident[:])

        gout_bf = sbt([P, Q * PACK], BF16, "gout_bf", after="key_pool")
        nc.vector.tensor_copy(*dealt_views(gout_bf, gout_raw[0], 0))
        val_scales = gather(val_bytes[:], U8, "val_scales", after="gout_raw0")
        nc.vector.tensor_copy(*dealt_views(gout_bf, gout_raw[1], 1))
        gout_words, gout_scales = quantise(gout_bf[:], "gout", Q)

        val_words = gather(val_pool[:].bitcast(U32), U32, "val_words")
        z = sbt([P, PACK], F32, "z", after="val_pool")
        nc.vector.tensor_reduce(z[:], z_terms[:].rearrange("p t r -> p r t"), mybir.AxisListType.X, ALU.add)
        inv_z = sbt([P, PACK], F32, "inv_z")
        inv_z2 = sbt([P, PACK], F32, "inv_z2")
        alpha = sbt([P, PACK], F32, "alpha")
        nc.vector.reciprocal(inv_z[:], z[:])
        nc.vector.tensor_tensor(inv_z2[:], inv_z[:], inv_z[:], ALU.mult)
        nc.vector.scalar_tensor_tensor(out=alpha[:], in0=qs_sb[:], scalar=2.0, in1=inv_z[:],
                                       op0=ALU.mult, op1=ALU.mult)

        qrows_bf = sbt([P, D * PACK], BF16, "qrows_bf")
        half_bf = HALF_COLS * PACK

        def cast_qrows(h):
            dst = qrows_bf[:, half_bf * h:half_bf * (h + 1)].rearrange("p (c i t) -> p c t i", i=4, t=PACK)
            src = qrows_raw[h][:].rearrange("p t (c i) -> p c t i", i=4)
            nc.scalar.copy(dst, src)

        cast_qrows(0)

        weighted = sbt([P, PACK, I], F32, "weighted")
        beta = sbt([P, PACK], F32, "beta")
        slope = sbt([P, PACK, I], F32, "slope")
        for r in range(PACK):
            c0 = wide_bank([P, I], "c0_%d" % r)
            nc.tensor.matmul_mx(out=c0[:], lhsT=gout_words[:, P * r:P * r + P].bitcast(FP8X4),
                                lhsT_scale=gout_scales[:, P * r:P * r + P],
                                rhs=val_words[:].bitcast(FP8X4), rhs_scale=val_scales[:], start=True, stop=True)
            nc.vector.scalar_tensor_tensor(out=weighted[:, r, :], in0=c0[:], scalar=inv_z2[:, r:r + 1],
                                           in1=parts[:, r, :], op0=ALU.mult, op1=ALU.mult,
                                           accum_out=beta[:, r:r + 1])
            nc.scalar.activation(slope[:, r, :], c0[:], ACT.Identity, bias=beta[:, r:r + 1],
                                 scale=alpha[:, r:r + 1])

        qrows_q = [quantise(qrows_bf[:, 0:half_bf], "qrows0", HALF_COLS)]
        cast_qrows(1)
        gs_bf = sbt([P, I * PACK], BF16, "gs_bf")
        for h in range(2):
            nc.vector.tensor_tensor(out=gs_bf[:, BANK * h:BANK * (h + 1)].rearrange("p (i r) -> p i r", r=PACK),
                                    in0=score[h][:].rearrange("p r i -> p i r"),
                                    in1=slope[:, :, P * h:P * h + P].rearrange("p r i -> p i r"), op=ALU.mult)
        gs_words = sbt([P, I], U32, "gs_words")
        gs_scales = sbt([P, I], U8, "gs_scales")
        for h in range(2):
            nc.vector.quantize_mx(out=gs_words[:, P * h:P * h + P].bitcast(FP8X4), scales=gs_scales[:, P * h:P * h + P],
                                  in_=gs_bf[:, BANK * h:BANK * (h + 1)])
        qrows_q.append(quantise(qrows_bf[:, half_bf:2 * half_bf], "qrows1", HALF_COLS, after="gs_bf"))

        fade_ps = wide_bank([P, P], "fade_ps")
        nc.tensor.transpose(fade_ps[:], fade_rows[:], ident[:])
        fade_col = sbt([P, CHUNKS], F32, "fade_col")
        nc.scalar.copy(fade_col[:], fade_ps[:, 0:CHUNKS])

        gks = []
        for j in range(TILES):
            words, scales = qrows_q[j // 2]
            cols = slice(P * (j % 2), P * (j % 2) + P)
            bank = score_bank([P, I], "gk_ps%d" % j)
            nc.tensor.matmul_mx(out=bank[:], lhsT=words[:, cols].bitcast(FP8X4), lhsT_scale=scales[:, cols],
                                rhs=gs_words[:].bitcast(FP8X4), rhs_scale=gs_scales[:], start=True, stop=True)
            gk = sbt([P, I], F32, "gk%d" % j)
            nc.scalar.copy(gk[:], bank[:])
            gks.append(gk)
        for j in range(TILES):
            nc.vector.tensor_copy(windows[j][:].indirect(places[:]), gks[j][:])

        def store(queue, j, half, res):
            queue.dma_start(out=out[P * j:P * j + P, BANK * half:BANK * (half + 1)], in_=res[:])

        faded = {}
        for c in range(CHUNKS):
            tiles = [j for j, half in TURNED if half == c // PACK]
            bank = wide_bank([P, len(tiles), P], "turn%d" % c)
            for n, j in enumerate(tiles):
                nc.tensor.transpose(bank[:, n, :], old_sb[j][:, P * c:P * c + P], ident[:])
            f = sbt([P, len(tiles), P], F32, "faded%d" % c)
            nc.scalar.activation(f[:], bank[:], ACT.Copy, scale=fade_col[:, c:c + 1])
            for n, j in enumerate(tiles):
                faded[j, c] = f[:, n, :]

        def gpsimd_share(j, width, queue, prod_after, res_after):
            prod = sbt([P, width], F32, "prod%d" % j, prod_after)
            nc.gpsimd.tensor_tensor(prod[:], old_sb[j][:, 0:width], fade_all[:, 0:width], ALU.mult)
            for half in range(width // BANK):
                cols = slice(BANK * half, BANK * (half + 1))
                res = sbt([P, BANK], F32, "res%d_%d" % (j, half), res_after)
                nc.gpsimd.tensor_tensor(res[:], prod[:, cols], windows[j][:, cols], ALU.add)
                store(queue, j, half, res)

        gpsimd_share(*GPSIMD_COLS[0], nc.sync, "qrows_bf", None)

        for n, (j, half) in enumerate(TURNED):
            bank = (back_bank if n < 2 else wide_bank)([P, PACK, P], "back%d" % n)
            for cc in range(PACK):
                nc.tensor.transpose(bank[:, cc, :], faded[j, PACK * half + cc], ident[:])
            res = sbt([P, BANK], F32, "res%d_%d" % (j, half), after="qrows_bf" if n == 0 else None)
            nc.vector.tensor_tensor(out=res[:], in0=bank[:].rearrange("p c n -> p (c n)"),
                                    in1=windows[j][:, BANK * half:BANK * (half + 1)], op=ALU.add)
            store(nc.sync, j, half, res)

        gpsimd_share(*GPSIMD_COLS[1], nc.scalar, "old0", "faded%d" % (CHUNKS - 1))
